import numpy as np
import ml_dtypes


def mxq(x, axis, fmt="e4m3"):
    dtype, down = {"e4m3": (ml_dtypes.float8_e4m3fn, 7), "e5m2": (ml_dtypes.float8_e5m2, 14)}[fmt]
    v = np.moveaxis(np.asarray(x, np.float32).astype(ml_dtypes.bfloat16).astype(np.float64), axis, -1)
    blocks = v.reshape(v.shape[:-1] + (-1, 32))
    amax = np.abs(blocks).max(-1, keepdims=True)
    byte = np.maximum(np.where(amax > 0, np.frexp(amax)[1] - 1 + 127, 0) - down, 1)
    scale = np.exp2(byte - 127.0)
    codes = (blocks / scale).astype(np.float32).astype(dtype).astype(np.float64)
    return np.moveaxis((codes * scale).reshape(v.shape), -1, axis)


WIDE = False


def mx_kscale(k, group=512):
    if not WIDE:
        return np.ones(k)
    levels = np.array([10, -10, 5, -5, 0])
    if group != 512:
        return np.exp2(np.random.permutation(np.resize(levels, k // group))).repeat(group)
    if k % 512:
        return np.exp2(np.random.permutation(np.resize(levels, k // 32))).repeat(32)
    a = np.empty((k // 512, 16))
    for p in range(k // 512):
        a[p, :8] = np.random.permutation(np.resize(levels, 8))
        for g in range(8):
            far = levels[np.abs(levels - a[p, g]) >= 10]
            a[p, g + 8] = far[np.random.randint(len(far))]
    return np.exp2(a.ravel()).repeat(32)


def f64(x):
    return np.asarray(x).astype(np.float64)


G, D, M, N = 2, 256, 128, 512


def setup_inputs():
    n = np.random.standard_normal
    s_d = mx_kscale(D, 0)
    return {
        "x": (n((G, D, M)) / s_d[:, None] / np.sqrt(D)).astype(np.float32),
        "c": (n((G, D, N)) * s_d[:, None] / np.sqrt(D)).astype(np.float32),
        "xn": (np.random.uniform(0.9, 1.3, (G, M, 1))).astype(np.float32),
        "cn": (np.random.uniform(0.9, 1.3, (G, 1, N))).astype(np.float32),
    }


def reference(x, c, xn, cn):
    xq = mxq(f64(x), 1, "e4m3")
    cq = mxq(f64(c), 1, "e4m3")
    z = xq.transpose(0, 2, 1) @ cq
    d2 = f64(xn) + f64(cn) - 2.0 * z
    y = 1.0 / ((1.0 + 0.25 * d2) * (1.0 + 0.25 * d2))
    return y

@@ -1,0 +1,184 @@
+from contextlib import ExitStack
+
+import concourse.mybir as mybir
+
+G, D, M, N = 2, 256, 128, 512
+FLOPS = 2 * G * D * M * N
+
+F32 = mybir.dt.float32
+BF16 = mybir.dt.bfloat16
+U32 = mybir.dt.uint32
+U8 = mybir.dt.uint8
+FP8X4 = mybir.dt.float8_e4m3fn_x4
+ACT = mybir.ActivationFunctionType
+ALU = mybir.AluOpType
+
+P = 128
+PACK = 4
+ROWS = 64
+W = 128
+CHUNKS = N // W
+SQ = 32
+LOADS = [128, 128, 128, 128]
+
+
+def tile_rows_kern_ratquad_kernel(tc, x, c, xn, cn, out):
+    nc = tc.nc
+    with ExitStack() as ctx:
+        sb = ctx.enter_context(tc.tile_pool(name="sb", bufs=1))
+        ps = ctx.enter_context(tc.psum_pool(name="ps", bufs=1))
+        ctx.enter_context(tc.manual_schedule())
+
+        cn_rows = sb.tile([P, SQ], F32, name="cn_rows", align_bytes=64)
+        cn_cols = sb.tile([P, SQ], F32, name="cn_cols", align_bytes=64)
+        xn_sb = sb.tile([P, G], F32, name="xn_sb")
+        row_term = sb.tile([P, G], F32, name="row_term")
+        x_raw = sb.tile([P, PACK, M], F32, name="x_raw")
+        x_bf = sb.tile([P, M * PACK], BF16, name="x_bf", align_bytes=64)
+        x_codes = sb.tile([P, M], U32, name="x_codes", align_bytes=64)
+        x_scales = sb.tile([P, M], U8, name="x_scales", align_bytes=64)
+
+        def per_chunk(label, shape, dtype):
+            return [sb.tile(shape, dtype, name="%s%d" % (label, k), align_bytes=64) for k in range(CHUNKS)]
+
+        c_bf = per_chunk("c_bf", [P, W * PACK], BF16)
+        c_codes = per_chunk("c_codes", [P, W], U32)
+        c_scales = per_chunk("c_scales", [P, W], U8)
+        cn_wide = per_chunk("cn_wide", [P, G * W], F32)
+        cn_all = per_chunk("cn_all", [P, G * W], F32)
+        v = per_chunk("v", [P, G * W], F32)
+        r1 = per_chunk("r1", [P, G * W], F32)
+        r2 = per_chunk("r2", [P, G * W], F32)
+        y = per_chunk("y", [P, G * W], F32)
+        z = [[ps.tile([M, W], F32, name="z%d_%d" % (g, k)) for k in range(CHUNKS)] for g in range(G)]
+
+        cn_src = cn.rearrange("g o (b j) -> (g o b) j", j=SQ)
+        nc.scalar.dma_start(out=cn_rows[:], in_=cn_src.unsqueeze(0).to_broadcast([P // SQ, SQ, SQ]))
+        with nc.allow_non_contiguous_dma(reason="one value a partition and group"):
+            nc.scalar.dma_start(out=xn_sb[:], in_=xn.rearrange("g m o -> m (g o)"))
+        nc.sync.dma_start(out=x_raw[:], in_=x.rearrange("g (p j) m -> (g p) j m", j=PACK))
+        c_view = c.rearrange("g (p j) n -> (g p) j n", j=PACK)
+        c_raw = []
+        first = 0
+        for width in LOADS:
+            landed = sb.tile([P, PACK, width], F32, name="c_raw%d" % first)
+            nc.sync.dma_start(out=landed[:], in_=c_view[:, :, first : first + width])
+            c_raw.extend(landed[:, :, a : a + W] for a in range(0, width, W))
+            first += width
+        warm = sb.tile([P, 2], F32, name="warm")
+        nc.gpsimd.memset(warm[:, 0:1], 1.0)
+        nc.scalar.activation(out=warm[:, 1:2], in_=warm[:, 0:1], func=ACT.Abs_reciprocal_sqrt)
+
+        def interleave(on_vector, dst, src):
+            dst4 = dst[:].rearrange("p (c i j) -> p c j i", i=4, j=PACK)
+            src4 = src.rearrange("p j (c i) -> p c j i", i=4)
+            if on_vector:
+                nc.vector.tensor_copy(out=dst4, in_=src4)
+            else:
+                nc.scalar.copy(out=dst4, in_=src4)
+
+        def quantize(codes, scales, src):
+            nc.vector.quantize_mx(out=codes[:].bitcast(FP8X4), scales=scales[:], in_=src[:])
+
+        def widen(on_vector, k):
+            blocks = W // SQ
+            src = cn_cols[:].rearrange("p (g b) -> p g b", g=G)[:, :, k * blocks : (k + 1) * blocks]
+            dst = cn_wide[k][:].rearrange("p (g b i) -> p g b i", g=G, i=SQ)
+            wide = src.unsqueeze(3).to_broadcast([P, G, blocks, SQ])
+            if on_vector:
+                nc.vector.tensor_scalar(out=dst, in0=wide, scalar1=0.5, scalar2=None, op0=ALU.mult)
+            else:
+                nc.scalar.activation(out=dst, in_=wide, func=ACT.Copy, scale=0.5)
+
+        def turn(k):
+            nc.vector.transpose(out=cn_all[k][:], in_=cn_wide[k][:])
+
+        def product(k):
+            for g in range(G):
+                rows = slice(g * ROWS, (g + 1) * ROWS)
+                nc.tensor.matmul_mx(
+                    out=z[g][k][:], lhsT=x_codes[rows, :].bitcast(FP8X4), lhsT_scale=x_scales[rows, :],
+                    rhs=c_codes[k][rows, :].bitcast(FP8X4), rhs_scale=c_scales[k][rows, :],
+                    start=True, stop=True)
+
+        def shift(k, g):
+            cols = slice(g * W, (g + 1) * W)
+            nc.vector.scalar_tensor_tensor(
+                out=v[k][:, cols], in0=z[g][k][:], scalar=row_term[:, g : g + 1], in1=cn_all[k][:, cols],
+                op0=ALU.subtract, op1=ALU.subtract)
+
+        def root(k, cols=slice(0, G * W)):
+            nc.scalar.activation(out=r1[k][:, cols], in_=v[k][:, cols], func=ACT.Abs_reciprocal_sqrt, scale=0.5)
+
+        def square(on_vector, dst, src, cols=slice(0, G * W)):
+            if on_vector:
+                nc.vector.tensor_tensor(out=dst[:, cols], in0=src[:, cols], in1=src[:, cols], op=ALU.mult)
+            else:
+                nc.scalar.activation(out=dst[:, cols], in_=src[:, cols], func=ACT.Square)
+
+        out_view = out.rearrange("g m n -> m g n")
+
+        def store(k, groups):
+            nc.sync.dma_start(out=out_view[:, groups, k * W : (k + 1) * W], in_=y[k][:].rearrange("p (g n) -> p g n", g=G)[:, groups, :])
+
+        nc.vector.transpose(out=cn_cols[:], in_=cn_rows[:])
+        widen(True, 0)
+        interleave(False, x_bf, x_raw[:])
+        widen(True, 1)
+        turn(0)
+        turn(1)
+        interleave(False, c_bf[0], c_raw[0])
+        quantize(x_codes, x_scales, x_bf)
+        nc.gpsimd.tensor_scalar(out=row_term[:], in0=xn_sb[:], scalar1=0.5, scalar2=2.0, op0=ALU.mult, op1=ALU.add)
+        interleave(True, c_bf[1], c_raw[1])
+        widen(False, 3)
+        widen(False, 2)
+        quantize(c_codes[0], c_scales[0], c_bf[0])
+        product(0)
+        quantize(c_codes[1], c_scales[1], c_bf[1])
+        interleave(True, c_bf[2], c_raw[2])
+        turn(2)
+        quantize(c_codes[2], c_scales[2], c_bf[2])
+        shift(0, 0)
+        product(1)
+        interleave(False, c_bf[3], c_raw[3])
+        shift(0, 1)
+        shift(1, 1)
+        shift(1, 0)
+        product(2)
+        root(0, slice(0 * W, 1 * W))
+        root(0, slice(1 * W, 2 * W))
+        quantize(c_codes[3], c_scales[3], c_bf[3])
+        root(1, slice(1 * W, 2 * W))
+        root(1, slice(0 * W, 1 * W))
+        turn(3)
+        square(False, r2[0], r1[0])
+        product(3)
+        shift(2, 1)
+        square(True, r2[1], r1[1], slice(1 * W, 2 * W))
+        shift(2, 0)
+        square(False, r2[1], r1[1], slice(0 * W, 1 * W))
+        root(2, slice(1 * W, 2 * W))
+        square(True, y[0], r2[0], slice(1 * W, 2 * W))
+        square(False, y[0], r2[0], slice(0 * W, 1 * W))
+        shift(3, 1)
+        shift(3, 0)
+        square(False, y[1], r2[1], slice(0 * W, 1 * W))
+        root(2, slice(0 * W, 1 * W))
+        square(True, y[1], r2[1], slice(1 * W, 2 * W))
+        store(0, slice(0, G))
+        square(True, r2[2], r1[2], slice(1 * W, 2 * W))
+        root(3, slice(1 * W, 2 * W))
+        root(3, slice(0 * W, 1 * W))
+        square(True, r2[2], r1[2], slice(0 * W, 1 * W))
+        store(1, slice(0, G))
+        square(True, y[2], r2[2], slice(1 * W, 2 * W))
+        square(False, r2[3], r1[3], slice(1 * W, 2 * W))
+        square(False, r2[3], r1[3], slice(0 * W, 1 * W))
+        square(True, y[2], r2[2], slice(0 * W, 1 * W))
+        store(2, slice(1, 2))
+        square(True, y[3], r2[3], slice(1 * W, 2 * W))
+        square(True, y[3], r2[3], slice(0 * W, 1 * W))
+        store(2, slice(0, 1))
+        store(3, slice(1, 2))
+        store(3, slice(0, 1))

@@ -29,10 +29,9 @@ def tile_rows_kern_ratquad_kernel(tc, x, c, xn, cn, out):
         ps = ctx.enter_context(tc.psum_pool(name="ps", bufs=1))
         ctx.enter_context(tc.manual_schedule())
 
-        cn_rows = sb.tile([P, SQ], F32, name="cn_rows", align_bytes=64)
-        cn_cols = sb.tile([P, SQ], F32, name="cn_cols", align_bytes=64)
+        cn_rows = sb.tile([P, W], F32, name="cn_rows", align_bytes=64)
+        cn_cols = sb.tile([P, W], F32, name="cn_cols", align_bytes=64)
         xn_sb = sb.tile([P, G], F32, name="xn_sb")
-        row_term = sb.tile([P, G], F32, name="row_term")
         x_raw = sb.tile([P, PACK, M], F32, name="x_raw")
         x_bf = sb.tile([P, M * PACK], BF16, name="x_bf", align_bytes=64)
         x_codes = sb.tile([P, M], U32, name="x_codes", align_bytes=64)
@@ -52,10 +51,8 @@ def tile_rows_kern_ratquad_kernel(tc, x, c, xn, cn, out):
         y = per_chunk("y", [P, G * W], F32)
         z = [[ps.tile([M, W], F32, name="z%d_%d" % (g, k)) for k in range(CHUNKS)] for g in range(G)]
 
-        cn_src = cn.rearrange("g o (b j) -> (g o b) j", j=SQ)
-        nc.scalar.dma_start(out=cn_rows[:], in_=cn_src.unsqueeze(0).to_broadcast([P // SQ, SQ, SQ]))
-        with nc.allow_non_contiguous_dma(reason="one value a partition and group"):
-            nc.scalar.dma_start(out=xn_sb[:], in_=xn.rearrange("g m o -> m (g o)"))
+        cn_src = cn.rearrange("g o (k n) -> (g o k) n", n=W)
+        nc.scalar.dma_start(out=cn_rows[:], in_=cn_src.unsqueeze(0).to_broadcast([P // (G * CHUNKS), G * CHUNKS, W]))
         nc.sync.dma_start(out=x_raw[:], in_=x.rearrange("g (p j) m -> (g p) j m", j=PACK))
         c_view = c.rearrange("g (p j) n -> (g p) j n", j=PACK)
         c_raw = []
@@ -65,8 +62,10 @@ def tile_rows_kern_ratquad_kernel(tc, x, c, xn, cn, out):
             nc.sync.dma_start(out=landed[:], in_=c_view[:, :, first : first + width])
             c_raw.extend(landed[:, :, a : a + W] for a in range(0, width, W))
             first += width
+        with nc.allow_non_contiguous_dma(reason="one value a partition and group"):
+            nc.sync.dma_start(out=xn_sb[:], in_=xn.rearrange("g m o -> m (g o)"))
         warm = sb.tile([P, 2], F32, name="warm")
-        nc.gpsimd.memset(warm[:, 0:1], 1.0)
+        nc.vector.memset(warm[:, 0:1], 1.0)
         nc.scalar.activation(out=warm[:, 1:2], in_=warm[:, 0:1], func=ACT.Abs_reciprocal_sqrt)
 
         def interleave(on_vector, dst, src):
@@ -82,13 +81,13 @@ def tile_rows_kern_ratquad_kernel(tc, x, c, xn, cn, out):
 
         def widen(on_vector, k):
             blocks = W // SQ
-            src = cn_cols[:].rearrange("p (g b) -> p g b", g=G)[:, :, k * blocks : (k + 1) * blocks]
+            src = cn_cols[:].rearrange("p (b r g k) -> p r k g b", b=blocks, g=G, k=CHUNKS)[:, 0, k, :, :]
             dst = cn_wide[k][:].rearrange("p (g b i) -> p g b i", g=G, i=SQ)
             wide = src.unsqueeze(3).to_broadcast([P, G, blocks, SQ])
             if on_vector:
-                nc.vector.tensor_scalar(out=dst, in0=wide, scalar1=0.5, scalar2=None, op0=ALU.mult)
+                nc.vector.tensor_scalar(out=dst, in0=wide, scalar1=4.0, scalar2=None, op0=ALU.add)
             else:
-                nc.scalar.activation(out=dst, in_=wide, func=ACT.Copy, scale=0.5)
+                nc.scalar.activation(out=dst, in_=wide, func=ACT.Copy, bias=4.0)
 
         def turn(k):
             nc.vector.transpose(out=cn_all[k][:], in_=cn_wide[k][:])
@@ -104,17 +103,18 @@ def tile_rows_kern_ratquad_kernel(tc, x, c, xn, cn, out):
         def shift(k, g):
             cols = slice(g * W, (g + 1) * W)
             nc.vector.scalar_tensor_tensor(
-                out=v[k][:, cols], in0=z[g][k][:], scalar=row_term[:, g : g + 1], in1=cn_all[k][:, cols],
-                op0=ALU.subtract, op1=ALU.subtract)
+                out=v[k][:, cols], in0=z[g][k][:], scalar=2.0, in1=cn_all[k][:, cols],
+                op0=ALU.mult, op1=ALU.subtract)
 
-        def root(k, cols=slice(0, G * W)):
-            nc.scalar.activation(out=r1[k][:, cols], in_=v[k][:, cols], func=ACT.Abs_reciprocal_sqrt, scale=0.5)
+        def root(k, g):
+            cols = slice(g * W, (g + 1) * W)
+            nc.scalar.activation(out=r1[k][:, cols], in_=v[k][:, cols], func=ACT.Abs_reciprocal_sqrt, scale=-1.0, bias=xn_sb[:, g : g + 1])
 
-        def square(on_vector, dst, src, cols=slice(0, G * W)):
+        def square(on_vector, dst, src, root_of_factor, cols=slice(0, G * W)):
             if on_vector:
-                nc.vector.tensor_tensor(out=dst[:, cols], in0=src[:, cols], in1=src[:, cols], op=ALU.mult)
+                nc.vector.scalar_tensor_tensor(out=dst[:, cols], in0=src[:, cols], scalar=root_of_factor * root_of_factor, in1=src[:, cols], op0=ALU.mult, op1=ALU.mult)
             else:
-                nc.scalar.activation(out=dst[:, cols], in_=src[:, cols], func=ACT.Square)
+                nc.scalar.activation(out=dst[:, cols], in_=src[:, cols], func=ACT.Square, scale=root_of_factor)
 
         out_view = out.rearrange("g m n -> m g n")
 
@@ -129,7 +129,6 @@ def tile_rows_kern_ratquad_kernel(tc, x, c, xn, cn, out):
         turn(1)
         interleave(False, c_bf[0], c_raw[0])
         quantize(x_codes, x_scales, x_bf)
-        nc.gpsimd.tensor_scalar(out=row_term[:], in0=xn_sb[:], scalar1=0.5, scalar2=2.0, op0=ALU.mult, op1=ALU.add)
         interleave(True, c_bf[1], c_raw[1])
         widen(False, 3)
         widen(False, 2)
@@ -146,39 +145,39 @@ def tile_rows_kern_ratquad_kernel(tc, x, c, xn, cn, out):
         shift(1, 1)
         shift(1, 0)
         product(2)
-        root(0, slice(0 * W, 1 * W))
-        root(0, slice(1 * W, 2 * W))
+        root(0, 0)
+        root(0, 1)
         quantize(c_codes[3], c_scales[3], c_bf[3])
-        root(1, slice(1 * W, 2 * W))
-        root(1, slice(0 * W, 1 * W))
+        root(1, 1)
+        root(1, 0)
         turn(3)
-        square(False, r2[0], r1[0])
+        square(False, r2[0], r1[0], 2.0)
         product(3)
         shift(2, 1)
-        square(True, r2[1], r1[1], slice(1 * W, 2 * W))
+        square(True, r2[1], r1[1], 2.0, slice(1 * W, 2 * W))
         shift(2, 0)
-        square(False, r2[1], r1[1], slice(0 * W, 1 * W))
-        root(2, slice(1 * W, 2 * W))
-        square(True, y[0], r2[0], slice(1 * W, 2 * W))
-        square(False, y[0], r2[0], slice(0 * W, 1 * W))
+        square(False, r2[1], r1[1], 2.0, slice(0 * W, 1 * W))
+        root(2, 1)
+        square(True, y[0], r2[0], 1.0, slice(1 * W, 2 * W))
+        square(False, y[0], r2[0], 1.0, slice(0 * W, 1 * W))
         shift(3, 1)
         shift(3, 0)
-        square(False, y[1], r2[1], slice(0 * W, 1 * W))
-        root(2, slice(0 * W, 1 * W))
-        square(True, y[1], r2[1], slice(1 * W, 2 * W))
+        square(False, y[1], r2[1], 1.0, slice(0 * W, 1 * W))
+        root(2, 0)
+        square(True, y[1], r2[1], 1.0, slice(1 * W, 2 * W))
         store(0, slice(0, G))
-        square(True, r2[2], r1[2], slice(1 * W, 2 * W))
-        root(3, slice(1 * W, 2 * W))
-        root(3, slice(0 * W, 1 * W))
-        square(True, r2[2], r1[2], slice(0 * W, 1 * W))
+        square(True, r2[2], r1[2], 2.0, slice(1 * W, 2 * W))
+        root(3, 1)
+        root(3, 0)
+        square(True, r2[2], r1[2], 2.0, slice(0 * W, 1 * W))
         store(1, slice(0, G))
-        square(True, y[2], r2[2], slice(1 * W, 2 * W))
-        square(False, r2[3], r1[3], slice(1 * W, 2 * W))
-        square(False, r2[3], r1[3], slice(0 * W, 1 * W))
-        square(True, y[2], r2[2], slice(0 * W, 1 * W))
+        square(True, y[2], r2[2], 1.0, slice(1 * W, 2 * W))
+        square(False, r2[3], r1[3], 2.0, slice(1 * W, 2 * W))
+        square(False, r2[3], r1[3], 2.0, slice(0 * W, 1 * W))
+        square(True, y[2], r2[2], 1.0, slice(0 * W, 1 * W))
         store(2, slice(1, 2))
-        square(True, y[3], r2[3], slice(1 * W, 2 * W))
-        square(True, y[3], r2[3], slice(0 * W, 1 * W))
+        square(True, y[3], r2[3], 1.0, slice(1 * W, 2 * W))
+        square(True, y[3], r2[3], 1.0, slice(0 * W, 1 * W))
         store(2, slice(0, 1))
         store(3, slice(1, 2))
         store(3, slice(0, 1))

from contextlib import ExitStack

import concourse.mybir as mybir

G, D, M, N = 2, 256, 128, 512
FLOPS = 2 * G * D * M * N

F32 = mybir.dt.float32
BF16 = mybir.dt.bfloat16
U32 = mybir.dt.uint32
U8 = mybir.dt.uint8
FP8X4 = mybir.dt.float8_e4m3fn_x4
ACT = mybir.ActivationFunctionType
ALU = mybir.AluOpType

P = 128
PACK = 4
ROWS = 64
W = 128
CHUNKS = N // W
SQ = 32
LOADS = [128, 128, 128, 128]


def tile_rows_kern_ratquad_kernel(tc, x, c, xn, cn, out):
    nc = tc.nc
    with ExitStack() as ctx:
        sb = ctx.enter_context(tc.tile_pool(name="sb", bufs=1))
        ps = ctx.enter_context(tc.psum_pool(name="ps", bufs=1))
        ctx.enter_context(tc.manual_schedule())

        cn_rows = sb.tile([P, W], F32, name="cn_rows", align_bytes=64)
        cn_cols = sb.tile([P, W], F32, name="cn_cols", align_bytes=64)
        xn_sb = sb.tile([P, G], F32, name="xn_sb")
        x_raw = sb.tile([P, PACK, M], F32, name="x_raw")
        x_bf = sb.tile([P, M * PACK], BF16, name="x_bf", align_bytes=64)
        x_codes = sb.tile([P, M], U32, name="x_codes", align_bytes=64)
        x_scales = sb.tile([P, M], U8, name="x_scales", align_bytes=64)

        def per_chunk(label, shape, dtype):
            return [sb.tile(shape, dtype, name="%s%d" % (label, k), align_bytes=64) for k in range(CHUNKS)]

        c_bf = per_chunk("c_bf", [P, W * PACK], BF16)
        c_codes = per_chunk("c_codes", [P, W], U32)
        c_scales = per_chunk("c_scales", [P, W], U8)
        cn_wide = per_chunk("cn_wide", [P, G * W], F32)
        cn_all = per_chunk("cn_all", [P, G * W], F32)
        v = per_chunk("v", [P, G * W], F32)
        r1 = per_chunk("r1", [P, G * W], F32)
        r2 = per_chunk("r2", [P, G * W], F32)
        y = per_chunk("y", [P, G * W], F32)
        z = [[ps.tile([M, W], F32, name="z%d_%d" % (g, k)) for k in range(CHUNKS)] for g in range(G)]

        cn_src = cn.rearrange("g o (k n) -> (g o k) n", n=W)
        nc.scalar.dma_start(out=cn_rows[:], in_=cn_src.unsqueeze(0).to_broadcast([P // (G * CHUNKS), G * CHUNKS, W]))
        nc.sync.dma_start(out=x_raw[:], in_=x.rearrange("g (p j) m -> (g p) j m", j=PACK))
        c_view = c.rearrange("g (p j) n -> (g p) j n", j=PACK)
        c_raw = []
        first = 0
        for width in LOADS:
            landed = sb.tile([P, PACK, width], F32, name="c_raw%d" % first)
            nc.sync.dma_start(out=landed[:], in_=c_view[:, :, first : first + width])
            c_raw.extend(landed[:, :, a : a + W] for a in range(0, width, W))
            first += width
        with nc.allow_non_contiguous_dma(reason="one value a partition and group"):
            nc.sync.dma_start(out=xn_sb[:], in_=xn.rearrange("g m o -> m (g o)"))
        warm = sb.tile([P, 2], F32, name="warm")
        nc.vector.memset(warm[:, 0:1], 1.0)
        nc.scalar.activation(out=warm[:, 1:2], in_=warm[:, 0:1], func=ACT.Abs_reciprocal_sqrt)

        def interleave(on_vector, dst, src):
            dst4 = dst[:].rearrange("p (c i j) -> p c j i", i=4, j=PACK)
            src4 = src.rearrange("p j (c i) -> p c j i", i=4)
            if on_vector:
                nc.vector.tensor_copy(out=dst4, in_=src4)
            else:
                nc.scalar.copy(out=dst4, in_=src4)

        def quantize(codes, scales, src):
            nc.vector.quantize_mx(out=codes[:].bitcast(FP8X4), scales=scales[:], in_=src[:])

        def widen(on_vector, k):
            blocks = W // SQ
            src = cn_cols[:].rearrange("p (b r g k) -> p r k g b", b=blocks, g=G, k=CHUNKS)[:, 0, k, :, :]
            dst = cn_wide[k][:].rearrange("p (g b i) -> p g b i", g=G, i=SQ)
            wide = src.unsqueeze(3).to_broadcast([P, G, blocks, SQ])
            if on_vector:
                nc.vector.tensor_scalar(out=dst, in0=wide, scalar1=4.0, scalar2=None, op0=ALU.add)
            else:
                nc.scalar.activation(out=dst, in_=wide, func=ACT.Copy, bias=4.0)

        def turn(k):
            nc.vector.transpose(out=cn_all[k][:], in_=cn_wide[k][:])

        def product(k):
            for g in range(G):
                rows = slice(g * ROWS, (g + 1) * ROWS)
                nc.tensor.matmul_mx(
                    out=z[g][k][:], lhsT=x_codes[rows, :].bitcast(FP8X4), lhsT_scale=x_scales[rows, :],
                    rhs=c_codes[k][rows, :].bitcast(FP8X4), rhs_scale=c_scales[k][rows, :],
                    start=True, stop=True)

        def shift(k, g):
            cols = slice(g * W, (g + 1) * W)
            nc.vector.scalar_tensor_tensor(
                out=v[k][:, cols], in0=z[g][k][:], scalar=2.0, in1=cn_all[k][:, cols],
                op0=ALU.mult, op1=ALU.subtract)

        def root(k, g):
            cols = slice(g * W, (g + 1) * W)
            nc.scalar.activation(out=r1[k][:, cols], in_=v[k][:, cols], func=ACT.Abs_reciprocal_sqrt, scale=-1.0, bias=xn_sb[:, g : g + 1])

        def square(on_vector, dst, src, root_of_factor, cols=slice(0, G * W)):
            if on_vector:
                nc.vector.scalar_tensor_tensor(out=dst[:, cols], in0=src[:, cols], scalar=root_of_factor * root_of_factor, in1=src[:, cols], op0=ALU.mult, op1=ALU.mult)
            else:
                nc.scalar.activation(out=dst[:, cols], in_=src[:, cols], func=ACT.Square, scale=root_of_factor)

        out_view = out.rearrange("g m n -> m g n")

        def store(k, groups):
            nc.sync.dma_start(out=out_view[:, groups, k * W : (k + 1) * W], in_=y[k][:].rearrange("p (g n) -> p g n", g=G)[:, groups, :])

        nc.vector.transpose(out=cn_cols[:], in_=cn_rows[:])
        widen(True, 0)
        interleave(False, x_bf, x_raw[:])
        widen(True, 1)
        turn(0)
        turn(1)
        interleave(False, c_bf[0], c_raw[0])
        quantize(x_codes, x_scales, x_bf)
        interleave(True, c_bf[1], c_raw[1])
        widen(False, 3)
        widen(False, 2)
        quantize(c_codes[0], c_scales[0], c_bf[0])
        product(0)
        quantize(c_codes[1], c_scales[1], c_bf[1])
        interleave(True, c_bf[2], c_raw[2])
        turn(2)
        quantize(c_codes[2], c_scales[2], c_bf[2])
        shift(0, 0)
        product(1)
        interleave(False, c_bf[3], c_raw[3])
        shift(0, 1)
        shift(1, 1)
        shift(1, 0)
        product(2)
        root(0, 0)
        root(0, 1)
        quantize(c_codes[3], c_scales[3], c_bf[3])
        root(1, 1)
        root(1, 0)
        turn(3)
        square(False, r2[0], r1[0], 2.0)
        product(3)
        shift(2, 1)
        square(True, r2[1], r1[1], 2.0, slice(1 * W, 2 * W))
        shift(2, 0)
        square(False, r2[1], r1[1], 2.0, slice(0 * W, 1 * W))
        root(2, 1)
        square(True, y[0], r2[0], 1.0, slice(1 * W, 2 * W))
        square(False, y[0], r2[0], 1.0, slice(0 * W, 1 * W))
        shift(3, 1)
        shift(3, 0)
        square(False, y[1], r2[1], 1.0, slice(0 * W, 1 * W))
        root(2, 0)
        square(True, y[1], r2[1], 1.0, slice(1 * W, 2 * W))
        store(0, slice(0, G))
        square(True, r2[2], r1[2], 2.0, slice(1 * W, 2 * W))
        root(3, 1)
        root(3, 0)
        square(True, r2[2], r1[2], 2.0, slice(0 * W, 1 * W))
        store(1, slice(0, G))
        square(True, y[2], r2[2], 1.0, slice(1 * W, 2 * W))
        square(False, r2[3], r1[3], 2.0, slice(1 * W, 2 * W))
        square(False, r2[3], r1[3], 2.0, slice(0 * W, 1 * W))
        square(True, y[2], r2[2], 1.0, slice(0 * W, 1 * W))
        store(2, slice(1, 2))
        square(True, y[3], r2[3], 1.0, slice(1 * W, 2 * W))
        square(True, y[3], r2[3], 1.0, slice(0 * W, 1 * W))
        store(2, slice(0, 1))
        store(3, slice(1, 2))
        store(3, slice(0, 1))
